import numpy as np
import ml_dtypes


def mxq(x, axis, fmt="e4m3"):
    dtype, down = {"e4m3": (ml_dtypes.float8_e4m3fn, 7), "e5m2": (ml_dtypes.float8_e5m2, 14)}[fmt]
    v = np.moveaxis(np.asarray(x, np.float32).astype(ml_dtypes.bfloat16).astype(np.float64), axis, -1)
    blocks = v.reshape(v.shape[:-1] + (-1, 32))
    amax = np.abs(blocks).max(-1, keepdims=True)
    byte = np.maximum(np.where(amax > 0, np.frexp(amax)[1] - 1 + 127, 0) - down, 1)
    scale = np.exp2(byte - 127.0)
    codes = (blocks / scale).astype(np.float32).astype(dtype).astype(np.float64)
    return np.moveaxis((codes * scale).reshape(v.shape), -1, axis)


WIDE = False


def mx_kscale(k):
    if not WIDE:
        return np.ones(k)
    levels = np.array([10, -10, 5, -5, 0])
    if k % 512:
        return np.exp2(np.random.permutation(np.resize(levels, k // 32))).repeat(32)
    a = np.empty((k // 512, 16))
    for p in range(k // 512):
        a[p, :8] = np.random.permutation(np.resize(levels, 8))
        for g in range(8):
            far = levels[np.abs(levels - a[p, g]) >= 10]
            a[p, g + 8] = far[np.random.randint(len(far))]
    return np.exp2(a.ravel()).repeat(32)


def f64(x):
    return np.asarray(x).astype(np.float64)


def striped8(idx):
    return np.concatenate([x.reshape(-1, 16).T for x in idx]).astype(np.uint16)


def runs(offs, k):
    lists = np.stack([offs[16 * r : 16 * r + 16].T.reshape(-1) for r in range(8)]).astype(np.int64)
    return lists[np.arange(k) % 512 // 64]


def pack_weight(w):
    k, n = w.shape
    w = f64(np.asarray(w, np.float32).astype(ml_dtypes.bfloat16)).reshape(k // 32, 32, n)
    amax = np.abs(w).max(1)
    byte = np.clip(np.where(amax > 0, np.frexp(amax)[1] - 1 + 127 - 7, 1), 1, 254)
    scaled = (w * np.exp2(127.0 - byte)[:, None, :]).reshape(k, n).astype(np.float32)
    words = np.ascontiguousarray(scaled.reshape(k // 512, 128, 4, n).transpose(0, 1, 3, 2)).astype(ml_dtypes.float8_e4m3fn).view(np.uint8)
    return words, np.ascontiguousarray(byte.astype(np.uint8).reshape(k // 512, 16, n))


def unpack_weight(words, scales):
    g, p, n, _ = words.shape
    vals = np.ascontiguousarray(words).view(ml_dtypes.float8_e4m3fn).astype(np.float64) * np.repeat(np.exp2(scales.astype(np.float64) - 127.0), 8, axis=1)[..., None]
    return vals.transpose(0, 1, 3, 2).reshape(g * 512, n)


E2M1 = np.array([0.0, 0.5, 1.0, 1.5, 2.0, 3.0, 4.0, 6.0, -0.0, -0.5, -1.0, -1.5, -2.0, -3.0, -4.0, -6.0])


def pack_fp4(w):
    k, n = w.shape
    w = f64(np.asarray(w, np.float32).astype(ml_dtypes.bfloat16)).reshape(k // 32, 32, n)
    amax = np.abs(w).max(1)
    mant, ex = np.frexp(amax / 6.0)
    byte = np.clip(np.where(amax > 0, np.where(mant > 0.5, ex, ex - 1) + 127, 1), 1, 254)
    scaled = (w * np.exp2(127.0 - byte)[:, None, :]).reshape(k, n).astype(np.float32)
    c = np.ascontiguousarray(scaled.reshape(k // 512, 128, 4, n).transpose(0, 1, 3, 2)).astype(ml_dtypes.float4_e2m1fn).view(np.uint8) & 0xF
    words = (c[..., 0::2] | (c[..., 1::2] << 4)).reshape(k // 512, 128, 2 * n)
    return np.ascontiguousarray(words), np.ascontiguousarray(byte.astype(np.uint8).reshape(k // 512, 16, n))


def unpack_fp4(words, scales):
    g, _, n = scales.shape
    words = np.ascontiguousarray(words).reshape(g, 128, n, 2)
    nib = np.empty((g, 128, n, 4), np.uint8)
    nib[..., 0::2] = words & 0xF
    nib[..., 1::2] = words >> 4
    vals = E2M1[nib] * np.repeat(np.exp2(scales.astype(np.float64) - 127.0), 8, axis=1)[..., None]
    return vals.transpose(0, 1, 3, 2).reshape(g * 512, n)


K, T, S, N, G, H, W = 512, 1024, 512, 512, 2048, 512, 256


def setup_inputs():
    n = np.random.standard_normal
    s = mx_kscale(K)[:, None]
    u = mx_kscale(S)
    packed_xT = pack_weight(n((K, T)) * s)
    packed_dT = pack_weight(n((K, G)) / s)
    packed_w1 = pack_fp4(n((H, N)) / np.sqrt(2 * H) / u[:, None])
    packed_w2 = pack_fp4(n((K, N)) / np.sqrt(2 * K) / s)
    return {
        "x_words": packed_xT[0],
        "x_scales": packed_xT[1],
        "d_words": packed_dT[0],
        "d_scales": packed_dT[1],
        "gn": (np.random.uniform(0.5, 1.5, (H, 1)) * u[:, None]).astype(np.float32),
        "w1_words": packed_w1[0],
        "w1_scales": packed_w1[1],
        "w2_words": packed_w2[0],
        "w2_scales": packed_w2[1],
        "offs": striped8(np.random.randint(0, T, (8, S))),
        "ka": striped8(np.random.randint(0, G, (8, H))),
        "kb": striped8(np.random.randint(0, G, (8, H))),
        "n1": striped8(np.stack([np.random.permutation(S)[:W] for _ in range(8)])),
        "n2": striped8(np.stack([np.random.permutation(S)[:W] for _ in range(8)])),
        "n3": striped8(np.stack([np.random.permutation(S) for _ in range(8)])),
        "hz": striped8(np.random.randint(0, T, (8, S))),
        "n4": striped8(np.stack([np.random.permutation(S) for _ in range(8)])),
        "n5": striped8(np.stack([np.random.permutation(S) for _ in range(8)])),
    }


def reference(x_words, x_scales, d_words, d_scales, gn, w1_words, w1_scales, w2_words, w2_scales, offs, ka, kb, n1, n2, n3, hz, n4, n5):
    d_ka = unpack_weight(d_words, d_scales)[np.arange(K)[:, None], runs(ka, K)]
    xq = unpack_weight(x_words, x_scales)[np.arange(K)[:, None], runs(offs, K)]
    d_kb = unpack_weight(d_words, d_scales)[np.arange(K)[:, None], runs(kb, K)]
    h = 0.0625 * (d_ka.T @ xq + d_kb.T @ xq)
    pa = h[np.arange(H)[:, None], runs(n2, H)]
    ds = h.copy()
    ds[np.arange(H)[:, None], runs(n1, H)] = pa
    z = f64(gn) * (ds - (0.5 * (ds[np.arange(H)[:, None], runs(n3, H)])))
    x_hz = unpack_weight(x_words, x_scales)[np.arange(K)[:, None], runs(hz, K)]
    h2 = unpack_fp4(w1_words, w1_scales).T @ mxq(z, 0, "e4m3") + unpack_fp4(w2_words, w2_scales).T @ x_hz
    ds2 = np.zeros((N, S))
    ds2[np.arange(N)[:, None], runs(n4, N)] = h2
    st = np.maximum(h2, ds2)
    ds3 = np.zeros((N, S))
    ds3[np.arange(N)[:, None], runs(n5, N)] = st
    return st - ds3

@@ -1,0 +1,226 @@
+from contextlib import ExitStack
+
+import concourse.mybir as mybir
+
+K, T, S, N, G, H, W = 512, 1024, 512, 512, 2048, 512, 256
+FLOPS = 4 * 2 * 512 * 512 * 512
+
+F32 = mybir.dt.float32
+BF16 = mybir.dt.bfloat16
+I32 = mybir.dt.int32
+U32 = mybir.dt.uint32
+U16 = mybir.dt.uint16
+U8 = mybir.dt.uint8
+FP8X4 = mybir.dt.float8_e4m3fn_x4
+FP4X4 = mybir.dt.float4_e2m1fn_x4
+ALU = mybir.AluOpType
+COPY = mybir.ActivationFunctionType.Copy
+
+P = 128
+TILES = 4
+HALF = S // 2
+HALVES = (slice(0, HALF), slice(HALF, S))
+LIST_HALVES = (slice(0, HALF // 16), slice(HALF // 16, S // 16))
+
+
+def tile_picked_ahznhksetsndtwin_none_p_kernel(
+    tc, x_words, x_scales, d_words, d_scales, gn, w1_words, w1_scales, w2_words, w2_scales,
+    offs, ka, kb, n1, n2, n3, hz, n4, n5, out,
+):
+    nc = tc.nc
+    with ExitStack() as ctx:
+        keep = ctx.enter_context(tc.tile_pool(name="keep", bufs=1))
+        psum = ctx.enter_context(tc.psum_pool(name="psum", bufs=1))
+
+        def load_list(src, name):
+            tile = keep.tile([P, src.shape[1]], U16, name=name)
+            nc.sync.dma_start(tile[:], src)
+            return tile
+
+        def zeroed_bytes(width, name):
+            tile = keep.tile([P, width], U8, name=name, align_bytes=64)
+            nc.vector.memset(tile[:].bitcast(I32), 0)
+            return tile
+
+        def place_scale_rows(dst, src):
+            for r in range(4):
+                nc.sync.dma_start(dst[r:P:32, :].bitcast(I32), src[8 * r : P : 32, :].bitcast(I32))
+
+        def load_scale_window(scales, width, name):
+            tile = keep.tile([P, width], U8, name=name)
+            rows = scales[0].bitcast(I32).unsqueeze(1).to_broadcast([16, 8, width // 4])
+            nc.sync.dma_start(tile[:].bitcast(I32), rows)
+            return tile
+
+        offs_l = load_list(offs, "offs_l")
+        x_sc = load_scale_window(x_scales, T, "x_sc")
+        ka_l = load_list(ka, "ka_l")
+        d_sc = load_scale_window(d_scales, G, "d_sc")
+        kb_l = load_list(kb, "kb_l")
+        d_w = keep.tile([P, G], I32, name="d_w")
+        nc.sync.dma_start(d_w[:], d_words[0].rearrange("p n t -> p (n t)").bitcast(I32))
+        x_w = keep.tile([P, T], I32, name="x_w")
+        nc.sync.dma_start(x_w[:], x_words[0].rearrange("p n t -> p (n t)").bitcast(I32))
+        plane = zeroed_bytes(2 * H + S, "plane")
+        hz_plane = zeroed_bytes(S, "hz_plane")
+        gain = keep.tile([P, TILES], F32, name="gain")
+        nc.sync.dma_start(gain[:], gn.rearrange("(p t) o -> p (t o)", t=TILES))
+        hz_l = load_list(hz, "hz_l")
+        n2_l = load_list(n2, "n2_l")
+        n1_l = load_list(n1, "n1_l")
+        n3_l = load_list(n3, "n3_l")
+        n4_l = load_list(n4, "n4_l")
+        n5_l = load_list(n5, "n5_l")
+        w_raw = keep.tile([P, 2, N // 2], I32, name="w_raw")
+        nc.sync.dma_start(w_raw[:, 0, :], w1_words[0].bitcast(I32))
+        nc.sync.dma_start(w_raw[:, 1, :], w2_words[0].bitcast(I32))
+        w_sc_raw = keep.tile([P, 2 * N], U8, name="w_sc_raw")
+        nc.gpsimd.memset(w_sc_raw[:].bitcast(I32), 0)
+        for i, scales in enumerate((w1_scales, w2_scales)):
+            for r in range(4):
+                nc.gpsimd.dma_start(w_sc_raw[r:P:32, i * N : (i + 1) * N].bitcast(I32), scales[0][r:16:4, :].bitcast(I32))
+
+        staged = keep.tile([P, 2 * H + S], U8, name="staged")
+        xq_b = keep.tile([P, S], U8, name="xq_b")
+        nc.vector.tensor_copy(xq_b[:], x_sc[:].indirect(offs_l[:]))
+        dq_b = keep.tile([P, 2 * H], U8, name="dq_b")
+        nc.vector.tensor_copy(dq_b[:, 0:H], d_sc[:].indirect(ka_l[:]))
+        nc.vector.tensor_copy(staged[:, 2 * H :].bitcast(I32), xq_b[:].bitcast(I32))
+        nc.vector.tensor_copy(dq_b[:, H : 2 * H], d_sc[:].indirect(kb_l[:]))
+        nc.vector.tensor_copy(
+            staged[:, 0 : 2 * H].rearrange("p (c t m) -> p c m t", c=2, t=TILES),
+            dq_b[:].rearrange("p (c m t) -> p c m t", c=2, t=TILES),
+        )
+        place_scale_rows(plane, staged)
+
+        dq_w = keep.tile([P, 2 * H], U32, name="dq_w", tag="picked_words", align_bytes=64)
+        dq_w_dealt = keep.tile([P, 2 * H], U32, name="dq_w_dealt", align_bytes=64)
+        for c, lst in enumerate((ka_l, kb_l)):
+            nc.vector.tensor_copy(dq_w[:, c * H : (c + 1) * H], d_w[:].bitcast(U32).indirect(lst[:]))
+        xq_w = keep.tile([P, S], U32, name="xq_w", align_bytes=64)
+        nc.vector.tensor_copy(xq_w[:, HALVES[0]], x_w[:].bitcast(U32).indirect(offs_l[:, LIST_HALVES[0]]))
+        nc.vector.tensor_copy(
+            dq_w_dealt[:].bitcast(I32).rearrange("p (c t m) -> p c m t", c=2, t=TILES),
+            dq_w[:].bitcast(I32).rearrange("p (c m t) -> p c m t", c=2, t=TILES),
+        )
+        nc.vector.tensor_copy(xq_w[:, HALVES[1]], x_w[:].bitcast(U32).indirect(offs_l[:, LIST_HALVES[1]]))
+
+        scale = keep.tile([P, TILES], F32, name="scale")
+        nc.scalar.mul(scale[:], gain[:], 0.0625)
+        w_dealt = keep.tile([P, 2 * 2 * N], U8, name="w_dealt", align_bytes=64)
+        nc.scalar.copy(
+            w_dealt[:].bitcast(U32).rearrange("p (i t a b) -> p i t a b", i=2, t=TILES, b=4),
+            w_raw[:].bitcast(U32).rearrange("p i (a t b) -> p i t a b", t=TILES, b=4),
+        )
+        w_plane = keep.tile([P, 2 * N], U8, name="w_plane", align_bytes=64)
+        nc.gpsimd.tensor_copy(
+            w_plane[:].bitcast(U32).rearrange("p (i t a b) -> p i t a b", i=2, t=TILES, b=2),
+            w_sc_raw[:].bitcast(U32).rearrange("p (i a t b) -> p i t a b", i=2, t=TILES, b=2),
+        )
+
+        ds = [keep.tile([P, S], F32, name="ds%d" % t) for t in range(TILES)]
+        pa = [keep.tile([P, W], F32, name="pa%d" % t, tag="pa%d" % t, align_bytes=64) for t in range(TILES)]
+
+        def first_product(t, cols, bank):
+            acc = psum.tile([P, cols.stop - cols.start], F32, name="h_ps%d" % bank, tag="bank%d" % bank)
+            for c in range(2):
+                rows = slice(c * H + t * P, c * H + (t + 1) * P)
+                nc.tensor.matmul_mx(
+                    out=acc[:], lhsT=dq_w_dealt[:, rows].bitcast(FP8X4), lhsT_scale=plane[:, rows],
+                    rhs=xq_w[:, cols].bitcast(FP8X4), rhs_scale=plane[:, 2 * H + cols.start : 2 * H + cols.stop],
+                    start=(c == 0), stop=(c == 1),
+                )
+            nc.scalar.activation(ds[t][:, cols], acc[:], COPY, scale=scale[:, t : t + 1])
+
+        for t in range(TILES):
+            if t == 0:
+                first_product(t, HALVES[0], TILES)
+                first_product(t, HALVES[1], t)
+                hz_b = keep.tile([P, S], U8, name="hz_b", tag="picked_words", align_bytes=64)
+                nc.vector.tensor_copy(hz_b[:], x_sc[:].indirect(hz_l[:]))
+                place_scale_rows(hz_plane, hz_b)
+            else:
+                first_product(t, slice(0, S), t)
+            nc.scalar.activation(pa[t][:], ds[t][:].indirect(n2_l[:]), COPY)
+            nc.vector.tensor_copy(ds[t][:].indirect(n1_l[:]), pa[t][:])
+        hz_w = keep.tile([P, S], U32, name="hz_w", tag="pa%d" % (TILES - 1), align_bytes=64)
+        nc.vector.tensor_copy(hz_w[:], x_w[:].bitcast(U32).indirect(hz_l[:]))
+
+        z_rows = [keep.tile([P, TILES, HALF], BF16, name="z_rows%d" % u) for u in range(2)]
+        for t in range(TILES):
+            for u in range(2):
+                moved = keep.tile([P, HALF], F32, name="moved%d_%d" % (t, u))
+                nc.scalar.activation(moved[:], ds[t][:].indirect(n3_l[:, LIST_HALVES[u]]), COPY)
+                nc.vector.scalar_tensor_tensor(z_rows[u][:, t, :], moved[:], -0.5, ds[t][:, HALVES[u]], ALU.mult, ALU.add)
+
+        z_w = keep.tile([P, S], U32, name="z_w", align_bytes=64)
+        z_plane = keep.tile([P, S], U8, name="z_plane", align_bytes=64)
+        h2 = [keep.tile([P, S], F32, name="h2_%d" % t) for t in range(TILES)]
+
+        def w_pass(i, t, acc, words, scales, start, stop):
+            first = i * N + t * P
+            nc.tensor.matmul_mx(
+                out=acc, lhsT=w_dealt[:, 2 * first : 2 * (first + P)].bitcast(FP4X4), lhsT_scale=w_plane[:, first : first + P],
+                rhs=words.bitcast(FP8X4), rhs_scale=scales, start=start, stop=stop,
+            )
+
+        first_halves = [psum.tile([P, HALF], F32, name="h2_ps0_%d" % u, tag="bank%d" % (TILES + 1 - u)) for u in range(2)]
+        h2_ps = [None] + [psum.tile([P, S], F32, name="h2_ps%d" % t, tag="bank%d" % ((TILES + 1 + t) % 8)) for t in range(1, TILES)]
+        for u in range(2):
+            w_pass(1, 0, first_halves[u][:], hz_w[:, HALVES[u]], hz_plane[:, HALVES[u]], True, False)
+        for t in range(1, TILES):
+            w_pass(1, t, h2_ps[t][:], hz_w[:], hz_plane[:], True, False)
+        for u in range(2):
+            cols = HALVES[u]
+            z_in = keep.tile([P, HALF, TILES], BF16, name="z_in%d" % u, align_bytes=64)
+            nc.vector.tensor_copy(
+                z_in[:].rearrange("p (c i) t -> p c t i", i=4), z_rows[u][:].rearrange("p t (c i) -> p c t i", i=4)
+            )
+            nc.vector.quantize_mx(
+                out=z_w[:, cols].bitcast(FP8X4), scales=z_plane[:, cols], in_=z_in[:].rearrange("p c t -> p (c t)")
+            )
+            w_pass(0, 0, first_halves[u][:], z_w[:, cols], z_plane[:, cols], False, True)
+            nc.scalar.copy(h2[0][:, cols], first_halves[u][:])
+            for t in range(1, TILES):
+                w_pass(0, t, h2_ps[t][:, cols], z_w[:, cols], z_plane[:, cols], False, u == 1)
+        for t in range(1, TILES):
+            nc.scalar.copy(h2[t][:], h2_ps[t][:])
+
+        out_rows = out.rearrange("(a t b) j -> t a b j", t=TILES, b=8)
+        ds2 = [keep.tile([P, 2 * S], F32, name="ds2_%d" % t) for t in range(TILES)]
+        ds3 = [keep.tile([P, 2 * S], F32, name="ds3_%d" % t) for t in range(TILES)]
+        st = [keep.tile([P, S], F32, name="st%d" % t) for t in range(TILES)]
+
+        def send_h2(t):
+            if t == 0:
+                for u in range(2):
+                    nc.vector.tensor_copy(ds2[t][:].indirect(n4_l[:, LIST_HALVES[u]]), h2[t][:, HALVES[u]])
+            else:
+                nc.vector.tensor_copy(ds2[t][:].indirect(n4_l[:]), h2[t][:])
+
+        def larger(t):
+            nc.vector.tensor_tensor(st[t][:], h2[t][:], ds2[t][:, 0:S], ALU.max)
+
+        def send_st(t):
+            nc.vector.tensor_copy(ds3[t][:].indirect(n5_l[:]), st[t][:])
+
+        def finish(t):
+            if t + 1 < TILES:
+                res = keep.tile([P, S], F32, name="res%d" % t)
+                nc.vector.tensor_tensor(res[:], st[t][:], ds3[t][:, 0:S], ALU.subtract)
+                nc.sync.dma_start(out_rows[t], res[:])
+            else:
+                for u, queue in enumerate((nc.sync, nc.scalar)):
+                    res = keep.tile([P, HALF], F32, name="res%d_%d" % (t, u))
+                    nc.vector.tensor_tensor(res[:], st[t][:, HALVES[u]], ds3[t][:, HALVES[u]], ALU.subtract)
+                    queue.dma_start(out_rows[t][:, :, HALVES[u]], res[:])
+
+        send_h2(0)
+        for t in range(TILES):
+            if t + 1 < TILES:
+                send_h2(t + 1)
+            larger(t)
+            if t > 0:
+                finish(t - 1)
+            send_st(t)
+        finish(TILES - 1)

@@ -150,8 +150,9 @@ def tile_picked_ahznhksetsndtwin_none_p_kernel(
         for t in range(TILES):
             for u in range(2):
                 moved = keep.tile([P, HALF], F32, name="moved%d_%d" % (t, u))
-                nc.scalar.activation(moved[:], ds[t][:].indirect(n3_l[:, LIST_HALVES[u]]), COPY)
-                nc.vector.scalar_tensor_tensor(z_rows[u][:, t, :], moved[:], -0.5, ds[t][:, HALVES[u]], ALU.mult, ALU.add)
+                nc.scalar.activation(moved[:], ds[t][:].indirect(n3_l[:, LIST_HALVES[u]]), COPY, scale=0.5)
+                engine = nc.gpsimd if t + 1 < TILES else nc.vector
+                engine.tensor_tensor(z_rows[u][:, t, :], ds[t][:, HALVES[u]], moved[:], ALU.subtract)
 
         z_w = keep.tile([P, S], U32, name="z_w", align_bytes=64)
         z_plane = keep.tile([P, S], U8, name="z_plane", align_bytes=64)
@@ -199,7 +200,11 @@ def tile_picked_ahznhksetsndtwin_none_p_kernel(
                 nc.vector.tensor_copy(ds2[t][:].indirect(n4_l[:]), h2[t][:])
 
         def larger(t):
-            nc.vector.tensor_tensor(st[t][:], h2[t][:], ds2[t][:, 0:S], ALU.max)
+            if t == 0:
+                for u in range(2):
+                    nc.vector.tensor_tensor(st[t][:, HALVES[u]], first_halves[u][:], ds2[t][:, HALVES[u]], ALU.max)
+            else:
+                nc.vector.tensor_tensor(st[t][:], h2_ps[t][:], ds2[t][:, 0:S], ALU.max)
 
         def send_st(t):
             nc.vector.tensor_copy(ds3[t][:].indirect(n5_l[:]), st[t][:])
@@ -207,7 +212,7 @@ def tile_picked_ahznhksetsndtwin_none_p_kernel(
         def finish(t):
             if t + 1 < TILES:
                 res = keep.tile([P, S], F32, name="res%d" % t)
-                nc.vector.tensor_tensor(res[:], st[t][:], ds3[t][:, 0:S], ALU.subtract)
+                nc.gpsimd.tensor_tensor(res[:], st[t][:], ds3[t][:, 0:S], ALU.subtract)
                 nc.sync.dma_start(out_rows[t], res[:])
             else:
                 for u, queue in enumerate((nc.sync, nc.scalar)):

@@ -15,11 +15,15 @@ FP8X4 = mybir.dt.float8_e4m3fn_x4
 FP4X4 = mybir.dt.float4_e2m1fn_x4
 ALU = mybir.AluOpType
 COPY = mybir.ActivationFunctionType.Copy
+RELU = mybir.ActivationFunctionType.Relu
 
 P = 128
 TILES = 4
 HALF = S // 2
 HALVES = (slice(0, HALF), slice(HALF, S))
+QUARTER = S // 4
+QUARTERS = (slice(0, QUARTER), slice(QUARTER, HALF))
+LIST_QUARTERS = (slice(0, QUARTER // 16), slice(QUARTER // 16, HALF // 16))
 LIST_HALVES = (slice(0, HALF // 16), slice(HALF // 16, S // 16))
 
 
@@ -62,7 +66,7 @@ def tile_picked_ahznhksetsndtwin_none_p_kernel(
         x_w = keep.tile([P, T], I32, name="x_w")
         nc.sync.dma_start(x_w[:], x_words[0].rearrange("p n t -> p (n t)").bitcast(I32))
         plane = zeroed_bytes(2 * H + S, "plane")
-        hz_plane = zeroed_bytes(S, "hz_plane")
+        hz_plane = [zeroed_bytes(HALF, "hz_plane%d" % u) for u in range(2)]
         gain = keep.tile([P, TILES], F32, name="gain")
         nc.sync.dma_start(gain[:], gn.rearrange("(p t) o -> p (t o)", t=TILES))
         hz_l = load_list(hz, "hz_l")
@@ -94,7 +98,7 @@ def tile_picked_ahznhksetsndtwin_none_p_kernel(
         place_scale_rows(plane, staged)
 
         dq_w = keep.tile([P, 2 * H], U32, name="dq_w", tag="picked_words", align_bytes=64)
-        dq_w_dealt = keep.tile([P, 2 * H], U32, name="dq_w_dealt", align_bytes=64)
+        dq_w_dealt = keep.tile([P, 2 * H], U32, name="dq_w_dealt", tag="dq_w_dealt", align_bytes=64)
         for c, lst in enumerate((ka_l, kb_l)):
             nc.vector.tensor_copy(dq_w[:, c * H : (c + 1) * H], d_w[:].bitcast(U32).indirect(lst[:]))
         xq_w = keep.tile([P, S], U32, name="xq_w", align_bytes=64)
@@ -112,12 +116,6 @@ def tile_picked_ahznhksetsndtwin_none_p_kernel(
             w_dealt[:].bitcast(U32).rearrange("p (i t a b) -> p i t a b", i=2, t=TILES, b=4),
             w_raw[:].bitcast(U32).rearrange("p i (a t b) -> p i t a b", t=TILES, b=4),
         )
-        w_plane = keep.tile([P, 2 * N], U8, name="w_plane", align_bytes=64)
-        nc.gpsimd.tensor_copy(
-            w_plane[:].bitcast(U32).rearrange("p (i t a b) -> p i t a b", i=2, t=TILES, b=2),
-            w_sc_raw[:].bitcast(U32).rearrange("p (i a t b) -> p i t a b", i=2, t=TILES, b=2),
-        )
-
         ds = [keep.tile([P, S], F32, name="ds%d" % t) for t in range(TILES)]
         pa = [keep.tile([P, W], F32, name="pa%d" % t, tag="pa%d" % t, align_bytes=64) for t in range(TILES)]
 
@@ -136,26 +134,47 @@ def tile_picked_ahznhksetsndtwin_none_p_kernel(
             if t == 0:
                 first_product(t, HALVES[0], TILES)
                 first_product(t, HALVES[1], t)
-                hz_b = keep.tile([P, S], U8, name="hz_b", tag="picked_words", align_bytes=64)
-                nc.vector.tensor_copy(hz_b[:], x_sc[:].indirect(hz_l[:]))
-                place_scale_rows(hz_plane, hz_b)
+                hz_b = keep.tile([P, HALF], U8, name="hz_b", tag="picked_words", align_bytes=64)
+                nc.vector.tensor_copy(hz_b[:], x_sc[:].indirect(hz_l[:, LIST_HALVES[0]]))
+                place_scale_rows(hz_plane[0], hz_b)
+                hz_w = keep.tile([P, HALF], U32, name="hz_w", align_bytes=64)
+                nc.vector.tensor_copy(hz_w[:], x_w[:].bitcast(U32).indirect(hz_l[:, LIST_HALVES[0]]))
             else:
                 first_product(t, slice(0, S), t)
-            nc.scalar.activation(pa[t][:], ds[t][:].indirect(n2_l[:]), COPY)
+            if t == 0:
+                nc.vector.tensor_copy(pa[t][:], ds[t][:].indirect(n2_l[:]))
+            else:
+                nc.scalar.activation(pa[t][:], ds[t][:].indirect(n2_l[:]), COPY)
             nc.vector.tensor_copy(ds[t][:].indirect(n1_l[:]), pa[t][:])
-        hz_w = keep.tile([P, S], U32, name="hz_w", tag="pa%d" % (TILES - 1), align_bytes=64)
-        nc.vector.tensor_copy(hz_w[:], x_w[:].bitcast(U32).indirect(hz_l[:]))
+        w_plane = keep.tile([P, 2 * N], U8, name="w_plane", tag="dq_w_dealt", align_bytes=64)
+        nc.gpsimd.tensor_copy(
+            w_plane[:].bitcast(U32).rearrange("p (i t a b) -> p i t a b", i=2, t=TILES, b=2),
+            w_sc_raw[:].bitcast(U32).rearrange("p (i a t b) -> p i t a b", i=2, t=TILES, b=2),
+        )
 
-        z_rows = [keep.tile([P, TILES, HALF], BF16, name="z_rows%d" % u) for u in range(2)]
-        for t in range(TILES):
-            for u in range(2):
-                moved = keep.tile([P, HALF], F32, name="moved%d_%d" % (t, u))
-                nc.scalar.activation(moved[:], ds[t][:].indirect(n3_l[:, LIST_HALVES[u]]), COPY, scale=0.5)
-                engine = nc.gpsimd if t + 1 < TILES else nc.vector
-                engine.tensor_tensor(z_rows[u][:, t, :], ds[t][:, HALVES[u]], moved[:], ALU.subtract)
 
-        z_w = keep.tile([P, S], U32, name="z_w", align_bytes=64)
-        z_plane = keep.tile([P, S], U8, name="z_plane", align_bytes=64)
+        z_rows = keep.tile([P, 2, TILES, QUARTER], BF16, name="z_rows")
+        for t in range(TILES - 1):
+            moved = keep.tile([P, HALF], F32, name="moved%d" % t)
+            nc.scalar.activation(moved[:], ds[t][:].indirect(n3_l[:, LIST_HALVES[0]]), COPY, scale=0.5)
+            nc.gpsimd.tensor_tensor(
+                z_rows[:, :, t, :], ds[t][:, HALVES[0]].rearrange("p (q c) -> p q c", q=2),
+                moved[:].rearrange("p (q c) -> p q c", q=2), ALU.subtract,
+            )
+        moved_late = [keep.tile([P, HALF], F32, name="moved_late%d" % t) for t in range(TILES - 1)]
+
+        def move_late(t):
+            nc.scalar.activation(moved_late[t][:], ds[t][:].indirect(n3_l[:, LIST_HALVES[1]]), COPY, scale=0.5)
+
+        move_late(0)
+        last = TILES - 1
+        for q in range(2):
+            moved = keep.tile([P, QUARTER], F32, name="moved_q%d" % q)
+            nc.scalar.activation(moved[:], ds[last][:].indirect(n3_l[:, LIST_QUARTERS[q]]), COPY, scale=0.5)
+            nc.vector.tensor_tensor(z_rows[:, q, last, :], ds[last][:, QUARTERS[q]], moved[:], ALU.subtract)
+        for t in range(1, last):
+            move_late(t)
+
         h2 = [keep.tile([P, S], F32, name="h2_%d" % t) for t in range(TILES)]
 
         def w_pass(i, t, acc, words, scales, start, stop):
@@ -165,52 +184,75 @@ def tile_picked_ahznhksetsndtwin_none_p_kernel(
                 rhs=words.bitcast(FP8X4), rhs_scale=scales, start=start, stop=stop,
             )
 
-        first_halves = [psum.tile([P, HALF], F32, name="h2_ps0_%d" % u, tag="bank%d" % (TILES + 1 - u)) for u in range(2)]
-        h2_ps = [None] + [psum.tile([P, S], F32, name="h2_ps%d" % t, tag="bank%d" % ((TILES + 1 + t) % 8)) for t in range(1, TILES)]
-        for u in range(2):
-            w_pass(1, 0, first_halves[u][:], hz_w[:, HALVES[u]], hz_plane[:, HALVES[u]], True, False)
+        def interleaved(dst, rows):
+            return dst.rearrange("p (c i) t -> p c t i", i=4), rows.rearrange("p t (c i) -> p c t i", i=4)
+
+        quarter_ps = [psum.tile([P, QUARTER], F32, name="quarter_ps%d" % q, tag="bank%d" % (5 + q)) for q in range(2)]
+        early_ps = [None] + [psum.tile([P, HALF], F32, name="early_ps%d" % t, tag="bank%d" % (7, 4, 0)[t - 1]) for t in range(1, TILES)]
+        for q in range(2):
+            w_pass(1, 0, quarter_ps[q][:], hz_w[:, QUARTERS[q]], hz_plane[0][:, QUARTERS[q]], True, False)
         for t in range(1, TILES):
-            w_pass(1, t, h2_ps[t][:], hz_w[:], hz_plane[:], True, False)
-        for u in range(2):
-            cols = HALVES[u]
-            z_in = keep.tile([P, HALF, TILES], BF16, name="z_in%d" % u, align_bytes=64)
-            nc.vector.tensor_copy(
-                z_in[:].rearrange("p (c i) t -> p c t i", i=4), z_rows[u][:].rearrange("p t (c i) -> p c t i", i=4)
-            )
+            w_pass(1, t, early_ps[t][:], hz_w[:], hz_plane[0][:], True, False)
+        z_in = [keep.tile([P, QUARTER, TILES], BF16, name="z_in%d" % q, tag="z_in%d" % q, align_bytes=64) for q in range(2)]
+        z_w = keep.tile([P, HALF], U32, name="z_w", align_bytes=64)
+        z_plane = keep.tile([P, HALF], U8, name="z_plane", tag="z_plane", align_bytes=64)
+        for q in range(2):
+            nc.vector.tensor_copy(*interleaved(z_in[q][:], z_rows[:, q]))
+        for q in range(2):
+            cols = QUARTERS[q]
             nc.vector.quantize_mx(
-                out=z_w[:, cols].bitcast(FP8X4), scales=z_plane[:, cols], in_=z_in[:].rearrange("p c t -> p (c t)")
+                out=z_w[:, cols].bitcast(FP8X4), scales=z_plane[:, cols], in_=z_in[q][:].rearrange("p c t -> p (c t)")
             )
-            w_pass(0, 0, first_halves[u][:], z_w[:, cols], z_plane[:, cols], False, True)
-            nc.scalar.copy(h2[0][:, cols], first_halves[u][:])
-            for t in range(1, TILES):
-                w_pass(0, t, h2_ps[t][:, cols], z_w[:, cols], z_plane[:, cols], False, u == 1)
+            w_pass(0, 0, quarter_ps[q][:], z_w[:, cols], z_plane[:, cols], False, True)
+            nc.scalar.copy(h2[0][:, cols], quarter_ps[q][:])
         for t in range(1, TILES):
-            nc.scalar.copy(h2[t][:], h2_ps[t][:])
+            w_pass(0, t, early_ps[t][:], z_w[:], z_plane[:], False, True)
+            nc.scalar.copy(h2[t][:, HALVES[0]], early_ps[t][:])
+
+        hz_b_late = keep.tile([P, HALF], U8, name="hz_b_late", tag="pa%d" % last, align_bytes=64)
+        nc.vector.tensor_copy(hz_b_late[:], x_sc[:].indirect(hz_l[:, LIST_HALVES[1]]))
+        place_scale_rows(hz_plane[1], hz_b_late)
+        hz_w_late = keep.tile([P, HALF], U32, name="hz_w_late", tag="z_in0", align_bytes=64)
+        nc.vector.tensor_copy(hz_w_late[:], x_w[:].bitcast(U32).indirect(hz_l[:, LIST_HALVES[1]]))
+        moved_late.append(keep.tile([P, HALF], F32, name="moved_last", tag="z_plane", align_bytes=64))
+        move_late(last)
+        ds2 = [keep.tile([P, 2 * S], F32, name="ds2_%d" % t) for t in range(TILES - 1)]
+        for q in range(2):
+            nc.vector.tensor_copy(ds2[0][:].indirect(n4_l[:, LIST_QUARTERS[q]]), h2[0][:, QUARTERS[q]])
+        for t in range(1, TILES - 1):
+            nc.vector.tensor_copy(ds2[t][:].indirect(n4_l[:, LIST_HALVES[0]]), h2[t][:, HALVES[0]])
+
+        z_rows_late = keep.tile([P, TILES, HALF], BF16, name="z_rows_late", tag="z_in1", align_bytes=64)
+        for t in range(TILES):
+            nc.gpsimd.tensor_tensor(z_rows_late[:, t, :], ds[t][:, HALVES[1]], moved_late[t][:], ALU.subtract)
+        z_in_late = keep.tile([P, HALF, TILES], BF16, name="z_in_late", align_bytes=64)
+        nc.scalar.copy(*interleaved(z_in_late[:], z_rows_late[:]))
+        z_w_late = keep.tile([P, HALF], U32, name="z_w_late", align_bytes=64)
+        z_plane_late = keep.tile([P, HALF], U8, name="z_plane_late", align_bytes=64)
+        nc.vector.quantize_mx(
+            out=z_w_late[:].bitcast(FP8X4), scales=z_plane_late[:], in_=z_in_late[:].rearrange("p c t -> p (c t)")
+        )
+        for t in range(TILES):
+            late_ps = psum.tile([P, HALF], F32, name="late_ps%d" % t, tag="bank%d" % (1, 2, 3, 5)[t])
+            w_pass(1, t, late_ps[:], hz_w_late[:], hz_plane[1][:], True, False)
+            w_pass(0, t, late_ps[:], z_w_late[:], z_plane_late[:], False, True)
+            nc.scalar.copy(h2[t][:, HALVES[1]], late_ps[:])
+        ds2.append(keep.tile([P, 2 * S], F32, name="ds2_last", tag="z_in1", align_bytes=64))
+        nc.vector.tensor_copy(ds2[last][:].indirect(n4_l[:, LIST_HALVES[0]]), h2[last][:, HALVES[0]])
 
         out_rows = out.rearrange("(a t b) j -> t a b j", t=TILES, b=8)
-        ds2 = [keep.tile([P, 2 * S], F32, name="ds2_%d" % t) for t in range(TILES)]
         ds3 = [keep.tile([P, 2 * S], F32, name="ds3_%d" % t) for t in range(TILES)]
         st = [keep.tile([P, S], F32, name="st%d" % t) for t in range(TILES)]
-
-        def send_h2(t):
-            if t == 0:
-                for u in range(2):
-                    nc.vector.tensor_copy(ds2[t][:].indirect(n4_l[:, LIST_HALVES[u]]), h2[t][:, HALVES[u]])
-            else:
-                nc.vector.tensor_copy(ds2[t][:].indirect(n4_l[:]), h2[t][:])
-
-        def larger(t):
-            if t == 0:
-                for u in range(2):
-                    nc.vector.tensor_tensor(st[t][:, HALVES[u]], first_halves[u][:], ds2[t][:, HALVES[u]], ALU.max)
-            else:
-                nc.vector.tensor_tensor(st[t][:], h2_ps[t][:], ds2[t][:, 0:S], ALU.max)
-
-        def send_st(t):
+        for t in range(TILES):
+            nc.vector.tensor_copy(ds2[t][:].indirect(n4_l[:, LIST_HALVES[1]]), h2[t][:, HALVES[1]])
+            rise = keep.tile([P, S], F32, name="rise%d" % t, tag="rise%d" % t if t < 2 else "gainful%d" % (t - 2))
+            nc.gpsimd.tensor_tensor(rise[:], ds2[t][:, 0:S], h2[t][:], ALU.subtract)
+            gainful = keep.tile([P, S], F32, name="gainful%d" % t, tag="gainful%d" % t if t < 2 else "rise%d" % (t - 2))
+            nc.scalar.activation(gainful[:], rise[:], RELU)
+            nc.gpsimd.tensor_tensor(st[t][:], h2[t][:], gainful[:], ALU.add)
+        for t in range(TILES):
             nc.vector.tensor_copy(ds3[t][:].indirect(n5_l[:]), st[t][:])
-
-        def finish(t):
-            if t + 1 < TILES:
+            if t < last:
                 res = keep.tile([P, S], F32, name="res%d" % t)
                 nc.gpsimd.tensor_tensor(res[:], st[t][:], ds3[t][:, 0:S], ALU.subtract)
                 nc.sync.dma_start(out_rows[t], res[:])
@@ -219,13 +261,3 @@ def tile_picked_ahznhksetsndtwin_none_p_kernel(
                     res = keep.tile([P, HALF], F32, name="res%d_%d" % (t, u))
                     nc.vector.tensor_tensor(res[:], st[t][:, HALVES[u]], ds3[t][:, HALVES[u]], ALU.subtract)
                     queue.dma_start(out_rows[t][:, :, HALVES[u]], res[:])
-
-        send_h2(0)
-        for t in range(TILES):
-            if t + 1 < TILES:
-                send_h2(t + 1)
-            larger(t)
-            if t > 0:
-                finish(t - 1)
-            send_st(t)
-        finish(TILES - 1)

@@ -3,7 +3,7 @@ from contextlib import ExitStack
 import concourse.mybir as mybir
 
 K, T, S, N, G, H, W = 512, 1024, 512, 512, 2048, 512, 256
-FLOPS = 4 * 2 * 512 * 512 * 512
+FLOPS = 2 * (2 * K * H * S) + 2 * H * N * S + 2 * K * N * S
 
 F32 = mybir.dt.float32
 BF16 = mybir.dt.bfloat16
@@ -19,12 +19,26 @@ RELU = mybir.ActivationFunctionType.Relu
 
 P = 128
 TILES = 4
+LAST = TILES - 1
+GROUP = 16
+QUADRANT = 32
+BLOCK = 8
+BLOCKS = P // BLOCK
+ROWS = QUADRANT // BLOCK
+RUN = 8
+WALK = 4
+
 HALF = S // 2
-HALVES = (slice(0, HALF), slice(HALF, S))
 QUARTER = S // 4
+HALVES = (slice(0, HALF), slice(HALF, S))
 QUARTERS = (slice(0, QUARTER), slice(QUARTER, HALF))
-LIST_QUARTERS = (slice(0, QUARTER // 16), slice(QUARTER // 16, HALF // 16))
-LIST_HALVES = (slice(0, HALF // 16), slice(HALF // 16, S // 16))
+LIST_HALVES = (slice(0, HALF // GROUP), slice(HALF // GROUP, S // GROUP))
+LIST_QUARTERS = (slice(0, QUARTER // GROUP), slice(QUARTER // GROUP, HALF // GROUP))
+
+FIRST_EARLY_BANK = 4
+QUARTER_BANKS = (5, 6)
+EARLY_BANKS = {1: 7, 2: 4, 3: 0}
+LATE_BANKS = (1, 2, 3, 5)
 
 
 def tile_picked_ahznhksetsndtwin_none_p_kernel(
@@ -41,20 +55,20 @@ def tile_picked_ahznhksetsndtwin_none_p_kernel(
             nc.sync.dma_start(tile[:], src)
             return tile
 
-        def zeroed_bytes(width, name):
+        def load_scale_window(scales, width, name):
+            tile = keep.tile([P, width], U8, name=name)
+            rows = scales[0].bitcast(I32).unsqueeze(1).to_broadcast([BLOCKS, BLOCK, width // 4])
+            nc.scalar.dma_start(tile[:].bitcast(I32), rows)
+            return tile
+
+        def zeroed_plane(width, name):
             tile = keep.tile([P, width], U8, name=name, align_bytes=64)
             nc.vector.memset(tile[:].bitcast(I32), 0)
             return tile
 
-        def place_scale_rows(dst, src):
-            for r in range(4):
-                nc.sync.dma_start(dst[r:P:32, :].bitcast(I32), src[8 * r : P : 32, :].bitcast(I32))
-
-        def load_scale_window(scales, width, name):
-            tile = keep.tile([P, width], U8, name=name)
-            rows = scales[0].bitcast(I32).unsqueeze(1).to_broadcast([16, 8, width // 4])
-            nc.sync.dma_start(tile[:].bitcast(I32), rows)
-            return tile
+        def place_scale_rows(plane, picked):
+            for r in range(ROWS):
+                nc.sync.dma_start(plane[r:P:QUADRANT, :].bitcast(I32), picked[BLOCK * r : P : QUADRANT, :].bitcast(I32))
 
         offs_l = load_list(offs, "offs_l")
         x_sc = load_scale_window(x_scales, T, "x_sc")
@@ -65,8 +79,8 @@ def tile_picked_ahznhksetsndtwin_none_p_kernel(
         nc.sync.dma_start(d_w[:], d_words[0].rearrange("p n t -> p (n t)").bitcast(I32))
         x_w = keep.tile([P, T], I32, name="x_w")
         nc.sync.dma_start(x_w[:], x_words[0].rearrange("p n t -> p (n t)").bitcast(I32))
-        plane = zeroed_bytes(2 * H + S, "plane")
-        hz_plane = [zeroed_bytes(HALF, "hz_plane%d" % u) for u in range(2)]
+        first_plane = zeroed_plane(2 * H + S, "first_plane")
+        hz_plane = [zeroed_plane(HALF, "hz_plane%d" % u) for u in range(2)]
         gain = keep.tile([P, TILES], F32, name="gain")
         nc.sync.dma_start(gain[:], gn.rearrange("(p t) o -> p (t o)", t=TILES))
         hz_l = load_list(hz, "hz_l")
@@ -81,26 +95,28 @@ def tile_picked_ahznhksetsndtwin_none_p_kernel(
         w_sc_raw = keep.tile([P, 2 * N], U8, name="w_sc_raw")
         nc.gpsimd.memset(w_sc_raw[:].bitcast(I32), 0)
         for i, scales in enumerate((w1_scales, w2_scales)):
-            for r in range(4):
-                nc.gpsimd.dma_start(w_sc_raw[r:P:32, i * N : (i + 1) * N].bitcast(I32), scales[0][r:16:4, :].bitcast(I32))
+            for r in range(ROWS):
+                nc.gpsimd.dma_start(
+                    w_sc_raw[r:P:QUADRANT, i * N : (i + 1) * N].bitcast(I32), scales[0][r:BLOCKS:ROWS, :].bitcast(I32)
+                )
 
         staged = keep.tile([P, 2 * H + S], U8, name="staged")
         xq_b = keep.tile([P, S], U8, name="xq_b")
         nc.vector.tensor_copy(xq_b[:], x_sc[:].indirect(offs_l[:]))
         dq_b = keep.tile([P, 2 * H], U8, name="dq_b")
         nc.vector.tensor_copy(dq_b[:, 0:H], d_sc[:].indirect(ka_l[:]))
-        nc.vector.tensor_copy(staged[:, 2 * H :].bitcast(I32), xq_b[:].bitcast(I32))
         nc.vector.tensor_copy(dq_b[:, H : 2 * H], d_sc[:].indirect(kb_l[:]))
+        nc.vector.tensor_copy(staged[:, 2 * H :].bitcast(I32), xq_b[:].bitcast(I32))
         nc.vector.tensor_copy(
             staged[:, 0 : 2 * H].rearrange("p (c t m) -> p c m t", c=2, t=TILES),
             dq_b[:].rearrange("p (c m t) -> p c m t", c=2, t=TILES),
         )
-        place_scale_rows(plane, staged)
+        place_scale_rows(first_plane, staged)
 
         dq_w = keep.tile([P, 2 * H], U32, name="dq_w", tag="picked_words", align_bytes=64)
         dq_w_dealt = keep.tile([P, 2 * H], U32, name="dq_w_dealt", tag="dq_w_dealt", align_bytes=64)
-        for c, lst in enumerate((ka_l, kb_l)):
-            nc.vector.tensor_copy(dq_w[:, c * H : (c + 1) * H], d_w[:].bitcast(U32).indirect(lst[:]))
+        for c, codes in enumerate((ka_l, kb_l)):
+            nc.vector.tensor_copy(dq_w[:, c * H : (c + 1) * H], d_w[:].bitcast(U32).indirect(codes[:]))
         xq_w = keep.tile([P, S], U32, name="xq_w", align_bytes=64)
         nc.vector.tensor_copy(xq_w[:, HALVES[0]], x_w[:].bitcast(U32).indirect(offs_l[:, LIST_HALVES[0]]))
         nc.vector.tensor_copy(
@@ -109,13 +125,14 @@ def tile_picked_ahznhksetsndtwin_none_p_kernel(
         )
         nc.vector.tensor_copy(xq_w[:, HALVES[1]], x_w[:].bitcast(U32).indirect(offs_l[:, LIST_HALVES[1]]))
 
-        scale = keep.tile([P, TILES], F32, name="scale")
-        nc.scalar.mul(scale[:], gain[:], 0.0625)
+        row_factor = keep.tile([P, TILES], F32, name="row_factor")
+        nc.scalar.mul(row_factor[:], gain[:], 0.0625)
         w_dealt = keep.tile([P, 2 * 2 * N], U8, name="w_dealt", align_bytes=64)
         nc.scalar.copy(
-            w_dealt[:].bitcast(U32).rearrange("p (i t a b) -> p i t a b", i=2, t=TILES, b=4),
-            w_raw[:].bitcast(U32).rearrange("p i (a t b) -> p i t a b", t=TILES, b=4),
+            w_dealt[:].bitcast(U32).rearrange("p (i t a b) -> p i t a b", i=2, t=TILES, b=RUN // 2),
+            w_raw[:].bitcast(U32).rearrange("p i (a t b) -> p i t a b", t=TILES, b=RUN // 2),
         )
+
         ds = [keep.tile([P, S], F32, name="ds%d" % t) for t in range(TILES)]
         pa = [keep.tile([P, W], F32, name="pa%d" % t, tag="pa%d" % t, align_bytes=64) for t in range(TILES)]
 
@@ -124,75 +141,76 @@ def tile_picked_ahznhksetsndtwin_none_p_kernel(
             for c in range(2):
                 rows = slice(c * H + t * P, c * H + (t + 1) * P)
                 nc.tensor.matmul_mx(
-                    out=acc[:], lhsT=dq_w_dealt[:, rows].bitcast(FP8X4), lhsT_scale=plane[:, rows],
-                    rhs=xq_w[:, cols].bitcast(FP8X4), rhs_scale=plane[:, 2 * H + cols.start : 2 * H + cols.stop],
+                    out=acc[:], lhsT=dq_w_dealt[:, rows].bitcast(FP8X4), lhsT_scale=first_plane[:, rows],
+                    rhs=xq_w[:, cols].bitcast(FP8X4), rhs_scale=first_plane[:, 2 * H + cols.start : 2 * H + cols.stop],
                     start=(c == 0), stop=(c == 1),
                 )
-            nc.scalar.activation(ds[t][:, cols], acc[:], COPY, scale=scale[:, t : t + 1])
+            nc.scalar.activation(ds[t][:, cols], acc[:], COPY, scale=row_factor[:, t : t + 1])
 
-        for t in range(TILES):
-            if t == 0:
-                first_product(t, HALVES[0], TILES)
-                first_product(t, HALVES[1], t)
-                hz_b = keep.tile([P, HALF], U8, name="hz_b", tag="picked_words", align_bytes=64)
-                nc.vector.tensor_copy(hz_b[:], x_sc[:].indirect(hz_l[:, LIST_HALVES[0]]))
-                place_scale_rows(hz_plane[0], hz_b)
-                hz_w = keep.tile([P, HALF], U32, name="hz_w", align_bytes=64)
-                nc.vector.tensor_copy(hz_w[:], x_w[:].bitcast(U32).indirect(hz_l[:, LIST_HALVES[0]]))
-            else:
-                first_product(t, slice(0, S), t)
-            if t == 0:
-                nc.vector.tensor_copy(pa[t][:], ds[t][:].indirect(n2_l[:]))
-            else:
-                nc.scalar.activation(pa[t][:], ds[t][:].indirect(n2_l[:]), COPY)
+        first_product(0, HALVES[0], FIRST_EARLY_BANK)
+        first_product(0, HALVES[1], 0)
+        hz_b = keep.tile([P, HALF], U8, name="hz_b", tag="picked_words", align_bytes=64)
+        nc.vector.tensor_copy(hz_b[:], x_sc[:].indirect(hz_l[:, LIST_HALVES[0]]))
+        place_scale_rows(hz_plane[0], hz_b)
+        hz_w = keep.tile([P, HALF], U32, name="hz_w", align_bytes=64)
+        nc.vector.tensor_copy(hz_w[:], x_w[:].bitcast(U32).indirect(hz_l[:, LIST_HALVES[0]]))
+        nc.vector.tensor_copy(pa[0][:], ds[0][:].indirect(n2_l[:]))
+        nc.vector.tensor_copy(ds[0][:].indirect(n1_l[:]), pa[0][:])
+        for t in range(1, TILES):
+            first_product(t, slice(0, S), t)
+            nc.scalar.activation(pa[t][:], ds[t][:].indirect(n2_l[:]), COPY)
             nc.vector.tensor_copy(ds[t][:].indirect(n1_l[:]), pa[t][:])
+
         w_plane = keep.tile([P, 2 * N], U8, name="w_plane", tag="dq_w_dealt", align_bytes=64)
         nc.gpsimd.tensor_copy(
-            w_plane[:].bitcast(U32).rearrange("p (i t a b) -> p i t a b", i=2, t=TILES, b=2),
-            w_sc_raw[:].bitcast(U32).rearrange("p (i a t b) -> p i t a b", i=2, t=TILES, b=2),
+            w_plane[:].bitcast(U32).rearrange("p (i t a b) -> p i t a b", i=2, t=TILES, b=RUN // 4),
+            w_sc_raw[:].bitcast(U32).rearrange("p (i a t b) -> p i t a b", i=2, t=TILES, b=RUN // 4),
         )
 
-
         z_rows = keep.tile([P, 2, TILES, QUARTER], BF16, name="z_rows")
-        for t in range(TILES - 1):
+        for t in range(LAST):
             moved = keep.tile([P, HALF], F32, name="moved%d" % t)
             nc.scalar.activation(moved[:], ds[t][:].indirect(n3_l[:, LIST_HALVES[0]]), COPY, scale=0.5)
             nc.gpsimd.tensor_tensor(
                 z_rows[:, :, t, :], ds[t][:, HALVES[0]].rearrange("p (q c) -> p q c", q=2),
                 moved[:].rearrange("p (q c) -> p q c", q=2), ALU.subtract,
             )
-        moved_late = [keep.tile([P, HALF], F32, name="moved_late%d" % t) for t in range(TILES - 1)]
+        moved_late = [keep.tile([P, HALF], F32, name="moved_late%d" % t) for t in range(LAST)]
 
-        def move_late(t):
+        def fetch_late(t):
             nc.scalar.activation(moved_late[t][:], ds[t][:].indirect(n3_l[:, LIST_HALVES[1]]), COPY, scale=0.5)
 
-        move_late(0)
-        last = TILES - 1
+        fetch_late(0)
         for q in range(2):
             moved = keep.tile([P, QUARTER], F32, name="moved_q%d" % q)
-            nc.scalar.activation(moved[:], ds[last][:].indirect(n3_l[:, LIST_QUARTERS[q]]), COPY, scale=0.5)
-            nc.vector.tensor_tensor(z_rows[:, q, last, :], ds[last][:, QUARTERS[q]], moved[:], ALU.subtract)
-        for t in range(1, last):
-            move_late(t)
+            nc.scalar.activation(moved[:], ds[LAST][:].indirect(n3_l[:, LIST_QUARTERS[q]]), COPY, scale=0.5)
+            nc.vector.tensor_tensor(z_rows[:, q, LAST, :], ds[LAST][:, QUARTERS[q]], moved[:], ALU.subtract)
+        for t in range(1, LAST):
+            fetch_late(t)
 
         h2 = [keep.tile([P, S], F32, name="h2_%d" % t) for t in range(TILES)]
 
-        def w_pass(i, t, acc, words, scales, start, stop):
+        def w_pass(i, t, acc, words, scales):
             first = i * N + t * P
             nc.tensor.matmul_mx(
-                out=acc, lhsT=w_dealt[:, 2 * first : 2 * (first + P)].bitcast(FP4X4), lhsT_scale=w_plane[:, first : first + P],
-                rhs=words.bitcast(FP8X4), rhs_scale=scales, start=start, stop=stop,
+                out=acc, lhsT=w_dealt[:, 2 * first : 2 * (first + P)].bitcast(FP4X4),
+                lhsT_scale=w_plane[:, first : first + P], rhs=words.bitcast(FP8X4), rhs_scale=scales,
+                start=(i == 1), stop=(i == 0),
             )
 
-        def interleaved(dst, rows):
-            return dst.rearrange("p (c i) t -> p c t i", i=4), rows.rearrange("p t (c i) -> p c t i", i=4)
+        def interleaved(words, rows):
+            return words.rearrange("p (c i) t -> p c t i", i=WALK), rows.rearrange("p t (c i) -> p c t i", i=WALK)
 
-        quarter_ps = [psum.tile([P, QUARTER], F32, name="quarter_ps%d" % q, tag="bank%d" % (5 + q)) for q in range(2)]
-        early_ps = [None] + [psum.tile([P, HALF], F32, name="early_ps%d" % t, tag="bank%d" % (7, 4, 0)[t - 1]) for t in range(1, TILES)]
+        quarter_ps = [
+            psum.tile([P, QUARTER], F32, name="quarter_ps%d" % q, tag="bank%d" % QUARTER_BANKS[q]) for q in range(2)
+        ]
+        early_ps = {
+            t: psum.tile([P, HALF], F32, name="early_ps%d" % t, tag="bank%d" % bank) for t, bank in EARLY_BANKS.items()
+        }
         for q in range(2):
-            w_pass(1, 0, quarter_ps[q][:], hz_w[:, QUARTERS[q]], hz_plane[0][:, QUARTERS[q]], True, False)
+            w_pass(1, 0, quarter_ps[q][:], hz_w[:, QUARTERS[q]], hz_plane[0][:, QUARTERS[q]])
         for t in range(1, TILES):
-            w_pass(1, t, early_ps[t][:], hz_w[:], hz_plane[0][:], True, False)
+            w_pass(1, t, early_ps[t][:], hz_w[:], hz_plane[0][:])
         z_in = [keep.tile([P, QUARTER, TILES], BF16, name="z_in%d" % q, tag="z_in%d" % q, align_bytes=64) for q in range(2)]
         z_w = keep.tile([P, HALF], U32, name="z_w", align_bytes=64)
         z_plane = keep.tile([P, HALF], U8, name="z_plane", tag="z_plane", align_bytes=64)
@@ -203,23 +221,24 @@ def tile_picked_ahznhksetsndtwin_none_p_kernel(
             nc.vector.quantize_mx(
                 out=z_w[:, cols].bitcast(FP8X4), scales=z_plane[:, cols], in_=z_in[q][:].rearrange("p c t -> p (c t)")
             )
-            w_pass(0, 0, quarter_ps[q][:], z_w[:, cols], z_plane[:, cols], False, True)
+            w_pass(0, 0, quarter_ps[q][:], z_w[:, cols], z_plane[:, cols])
             nc.scalar.copy(h2[0][:, cols], quarter_ps[q][:])
         for t in range(1, TILES):
-            w_pass(0, t, early_ps[t][:], z_w[:], z_plane[:], False, True)
+            w_pass(0, t, early_ps[t][:], z_w[:], z_plane[:])
             nc.scalar.copy(h2[t][:, HALVES[0]], early_ps[t][:])
 
-        hz_b_late = keep.tile([P, HALF], U8, name="hz_b_late", tag="pa%d" % last, align_bytes=64)
+        hz_b_late = keep.tile([P, HALF], U8, name="hz_b_late", tag="pa%d" % LAST, align_bytes=64)
         nc.vector.tensor_copy(hz_b_late[:], x_sc[:].indirect(hz_l[:, LIST_HALVES[1]]))
         place_scale_rows(hz_plane[1], hz_b_late)
         hz_w_late = keep.tile([P, HALF], U32, name="hz_w_late", tag="z_in0", align_bytes=64)
         nc.vector.tensor_copy(hz_w_late[:], x_w[:].bitcast(U32).indirect(hz_l[:, LIST_HALVES[1]]))
         moved_late.append(keep.tile([P, HALF], F32, name="moved_last", tag="z_plane", align_bytes=64))
-        move_late(last)
-        ds2 = [keep.tile([P, 2 * S], F32, name="ds2_%d" % t) for t in range(TILES - 1)]
+        fetch_late(LAST)
+
+        ds2 = [keep.tile([P, S], F32, name="ds2_%d" % t) for t in range(LAST)]
         for q in range(2):
             nc.vector.tensor_copy(ds2[0][:].indirect(n4_l[:, LIST_QUARTERS[q]]), h2[0][:, QUARTERS[q]])
-        for t in range(1, TILES - 1):
+        for t in range(1, LAST):
             nc.vector.tensor_copy(ds2[t][:].indirect(n4_l[:, LIST_HALVES[0]]), h2[t][:, HALVES[0]])
 
         z_rows_late = keep.tile([P, TILES, HALF], BF16, name="z_rows_late", tag="z_in1", align_bytes=64)
@@ -233,31 +252,32 @@ def tile_picked_ahznhksetsndtwin_none_p_kernel(
             out=z_w_late[:].bitcast(FP8X4), scales=z_plane_late[:], in_=z_in_late[:].rearrange("p c t -> p (c t)")
         )
         for t in range(TILES):
-            late_ps = psum.tile([P, HALF], F32, name="late_ps%d" % t, tag="bank%d" % (1, 2, 3, 5)[t])
-            w_pass(1, t, late_ps[:], hz_w_late[:], hz_plane[1][:], True, False)
-            w_pass(0, t, late_ps[:], z_w_late[:], z_plane_late[:], False, True)
+            late_ps = psum.tile([P, HALF], F32, name="late_ps%d" % t, tag="bank%d" % LATE_BANKS[t])
+            w_pass(1, t, late_ps[:], hz_w_late[:], hz_plane[1][:])
+            w_pass(0, t, late_ps[:], z_w_late[:], z_plane_late[:])
             nc.scalar.copy(h2[t][:, HALVES[1]], late_ps[:])
-        ds2.append(keep.tile([P, 2 * S], F32, name="ds2_last", tag="z_in1", align_bytes=64))
-        nc.vector.tensor_copy(ds2[last][:].indirect(n4_l[:, LIST_HALVES[0]]), h2[last][:, HALVES[0]])
+        ds2.append(keep.tile([P, S], F32, name="ds2_last", tag="z_in1", align_bytes=64))
+        nc.vector.tensor_copy(ds2[LAST][:].indirect(n4_l[:, LIST_HALVES[0]]), h2[LAST][:, HALVES[0]])
 
-        out_rows = out.rearrange("(a t b) j -> t a b j", t=TILES, b=8)
+        out_rows = out.rearrange("(a t b) j -> t a b j", t=TILES, b=RUN)
         ds3 = [keep.tile([P, 2 * S], F32, name="ds3_%d" % t) for t in range(TILES)]
         st = [keep.tile([P, S], F32, name="st%d" % t) for t in range(TILES)]
         for t in range(TILES):
+            tags = ("rise%d" % (t % 2), "excess%d" % (t % 2))
             nc.vector.tensor_copy(ds2[t][:].indirect(n4_l[:, LIST_HALVES[1]]), h2[t][:, HALVES[1]])
-            rise = keep.tile([P, S], F32, name="rise%d" % t, tag="rise%d" % t if t < 2 else "gainful%d" % (t - 2))
-            nc.gpsimd.tensor_tensor(rise[:], ds2[t][:, 0:S], h2[t][:], ALU.subtract)
-            gainful = keep.tile([P, S], F32, name="gainful%d" % t, tag="gainful%d" % t if t < 2 else "rise%d" % (t - 2))
-            nc.scalar.activation(gainful[:], rise[:], RELU)
-            nc.gpsimd.tensor_tensor(st[t][:], h2[t][:], gainful[:], ALU.add)
-        for t in range(TILES):
+            rise = keep.tile([P, S], F32, name="rise%d" % t, tag=tags[t // 2])
+            nc.gpsimd.tensor_tensor(rise[:], ds2[t][:], h2[t][:], ALU.subtract)
+            excess = keep.tile([P, S], F32, name="excess%d" % t, tag=tags[1 - t // 2])
+            nc.scalar.activation(excess[:], rise[:], RELU)
+            nc.gpsimd.tensor_tensor(st[t][:], h2[t][:], excess[:], ALU.add)
+
+        for t in range(LAST):
             nc.vector.tensor_copy(ds3[t][:].indirect(n5_l[:]), st[t][:])
-            if t < last:
-                res = keep.tile([P, S], F32, name="res%d" % t)
-                nc.gpsimd.tensor_tensor(res[:], st[t][:], ds3[t][:, 0:S], ALU.subtract)
-                nc.sync.dma_start(out_rows[t], res[:])
-            else:
-                for u, queue in enumerate((nc.sync, nc.scalar)):
-                    res = keep.tile([P, HALF], F32, name="res%d_%d" % (t, u))
-                    nc.vector.tensor_tensor(res[:], st[t][:, HALVES[u]], ds3[t][:, HALVES[u]], ALU.subtract)
-                    queue.dma_start(out_rows[t][:, :, HALVES[u]], res[:])
+            result = keep.tile([P, S], F32, name="result%d" % t)
+            nc.gpsimd.tensor_tensor(result[:], st[t][:], ds3[t][:, 0:S], ALU.subtract)
+            nc.sync.dma_start(out_rows[t], result[:])
+        nc.vector.tensor_copy(ds3[LAST][:].indirect(n5_l[:]), st[LAST][:])
+        for u, queue in enumerate((nc.sync, nc.scalar)):
+            result = keep.tile([P, HALF], F32, name="last_result%d" % u)
+            nc.vector.tensor_tensor(result[:], st[LAST][:, HALVES[u]], ds3[LAST][:, HALVES[u]], ALU.subtract)
+            queue.dma_start(out_rows[LAST][:, :, HALVES[u]], result[:])

from contextlib import ExitStack

import concourse.mybir as mybir

K, T, S, N, G, H, W = 512, 1024, 512, 512, 2048, 512, 256
FLOPS = 2 * (2 * K * H * S) + 2 * H * N * S + 2 * K * N * S

F32 = mybir.dt.float32
BF16 = mybir.dt.bfloat16
I32 = mybir.dt.int32
U32 = mybir.dt.uint32
U16 = mybir.dt.uint16
U8 = mybir.dt.uint8
FP8X4 = mybir.dt.float8_e4m3fn_x4
FP4X4 = mybir.dt.float4_e2m1fn_x4
ALU = mybir.AluOpType
COPY = mybir.ActivationFunctionType.Copy
RELU = mybir.ActivationFunctionType.Relu

P = 128
TILES = 4
LAST = TILES - 1
GROUP = 16
QUADRANT = 32
BLOCK = 8
BLOCKS = P // BLOCK
ROWS = QUADRANT // BLOCK
RUN = 8
WALK = 4

HALF = S // 2
QUARTER = S // 4
HALVES = (slice(0, HALF), slice(HALF, S))
QUARTERS = (slice(0, QUARTER), slice(QUARTER, HALF))
LIST_HALVES = (slice(0, HALF // GROUP), slice(HALF // GROUP, S // GROUP))
LIST_QUARTERS = (slice(0, QUARTER // GROUP), slice(QUARTER // GROUP, HALF // GROUP))

FIRST_EARLY_BANK = 4
QUARTER_BANKS = (5, 6)
EARLY_BANKS = {1: 7, 2: 4, 3: 0}
LATE_BANKS = (1, 2, 3, 5)


def tile_picked_ahznhksetsndtwin_none_p_kernel(
    tc, x_words, x_scales, d_words, d_scales, gn, w1_words, w1_scales, w2_words, w2_scales,
    offs, ka, kb, n1, n2, n3, hz, n4, n5, out,
):
    nc = tc.nc
    with ExitStack() as ctx:
        keep = ctx.enter_context(tc.tile_pool(name="keep", bufs=1))
        psum = ctx.enter_context(tc.psum_pool(name="psum", bufs=1))

        def load_list(src, name):
            tile = keep.tile([P, src.shape[1]], U16, name=name)
            nc.sync.dma_start(tile[:], src)
            return tile

        def load_scale_window(scales, width, name):
            tile = keep.tile([P, width], U8, name=name)
            rows = scales[0].bitcast(I32).unsqueeze(1).to_broadcast([BLOCKS, BLOCK, width // 4])
            nc.scalar.dma_start(tile[:].bitcast(I32), rows)
            return tile

        def zeroed_plane(width, name):
            tile = keep.tile([P, width], U8, name=name, align_bytes=64)
            nc.vector.memset(tile[:].bitcast(I32), 0)
            return tile

        def place_scale_rows(plane, picked):
            for r in range(ROWS):
                nc.sync.dma_start(plane[r:P:QUADRANT, :].bitcast(I32), picked[BLOCK * r : P : QUADRANT, :].bitcast(I32))

        offs_l = load_list(offs, "offs_l")
        x_sc = load_scale_window(x_scales, T, "x_sc")
        ka_l = load_list(ka, "ka_l")
        d_sc = load_scale_window(d_scales, G, "d_sc")
        kb_l = load_list(kb, "kb_l")
        d_w = keep.tile([P, G], I32, name="d_w")
        nc.sync.dma_start(d_w[:], d_words[0].rearrange("p n t -> p (n t)").bitcast(I32))
        x_w = keep.tile([P, T], I32, name="x_w")
        nc.sync.dma_start(x_w[:], x_words[0].rearrange("p n t -> p (n t)").bitcast(I32))
        first_plane = zeroed_plane(2 * H + S, "first_plane")
        hz_plane = [zeroed_plane(HALF, "hz_plane%d" % u) for u in range(2)]
        gain = keep.tile([P, TILES], F32, name="gain")
        nc.sync.dma_start(gain[:], gn.rearrange("(p t) o -> p (t o)", t=TILES))
        hz_l = load_list(hz, "hz_l")
        n2_l = load_list(n2, "n2_l")
        n1_l = load_list(n1, "n1_l")
        n3_l = load_list(n3, "n3_l")
        n4_l = load_list(n4, "n4_l")
        n5_l = load_list(n5, "n5_l")
        w_raw = keep.tile([P, 2, N // 2], I32, name="w_raw")
        nc.sync.dma_start(w_raw[:, 0, :], w1_words[0].bitcast(I32))
        nc.sync.dma_start(w_raw[:, 1, :], w2_words[0].bitcast(I32))
        w_sc_raw = keep.tile([P, 2 * N], U8, name="w_sc_raw")
        nc.gpsimd.memset(w_sc_raw[:].bitcast(I32), 0)
        for i, scales in enumerate((w1_scales, w2_scales)):
            for r in range(ROWS):
                nc.gpsimd.dma_start(
                    w_sc_raw[r:P:QUADRANT, i * N : (i + 1) * N].bitcast(I32), scales[0][r:BLOCKS:ROWS, :].bitcast(I32)
                )

        staged = keep.tile([P, 2 * H + S], U8, name="staged")
        xq_b = keep.tile([P, S], U8, name="xq_b")
        nc.vector.tensor_copy(xq_b[:], x_sc[:].indirect(offs_l[:]))
        dq_b = keep.tile([P, 2 * H], U8, name="dq_b")
        nc.vector.tensor_copy(dq_b[:, 0:H], d_sc[:].indirect(ka_l[:]))
        nc.vector.tensor_copy(dq_b[:, H : 2 * H], d_sc[:].indirect(kb_l[:]))
        nc.vector.tensor_copy(staged[:, 2 * H :].bitcast(I32), xq_b[:].bitcast(I32))
        nc.vector.tensor_copy(
            staged[:, 0 : 2 * H].rearrange("p (c t m) -> p c m t", c=2, t=TILES),
            dq_b[:].rearrange("p (c m t) -> p c m t", c=2, t=TILES),
        )
        place_scale_rows(first_plane, staged)

        dq_w = keep.tile([P, 2 * H], U32, name="dq_w", tag="picked_words", align_bytes=64)
        dq_w_dealt = keep.tile([P, 2 * H], U32, name="dq_w_dealt", tag="dq_w_dealt", align_bytes=64)
        for c, codes in enumerate((ka_l, kb_l)):
            nc.vector.tensor_copy(dq_w[:, c * H : (c + 1) * H], d_w[:].bitcast(U32).indirect(codes[:]))
        xq_w = keep.tile([P, S], U32, name="xq_w", align_bytes=64)
        nc.vector.tensor_copy(xq_w[:, HALVES[0]], x_w[:].bitcast(U32).indirect(offs_l[:, LIST_HALVES[0]]))
        nc.vector.tensor_copy(
            dq_w_dealt[:].bitcast(I32).rearrange("p (c t m) -> p c m t", c=2, t=TILES),
            dq_w[:].bitcast(I32).rearrange("p (c m t) -> p c m t", c=2, t=TILES),
        )
        nc.vector.tensor_copy(xq_w[:, HALVES[1]], x_w[:].bitcast(U32).indirect(offs_l[:, LIST_HALVES[1]]))

        row_factor = keep.tile([P, TILES], F32, name="row_factor")
        nc.scalar.mul(row_factor[:], gain[:], 0.0625)
        w_dealt = keep.tile([P, 2 * 2 * N], U8, name="w_dealt", align_bytes=64)
        nc.scalar.copy(
            w_dealt[:].bitcast(U32).rearrange("p (i t a b) -> p i t a b", i=2, t=TILES, b=RUN // 2),
            w_raw[:].bitcast(U32).rearrange("p i (a t b) -> p i t a b", t=TILES, b=RUN // 2),
        )

        ds = [keep.tile([P, S], F32, name="ds%d" % t) for t in range(TILES)]
        pa = [keep.tile([P, W], F32, name="pa%d" % t, tag="pa%d" % t, align_bytes=64) for t in range(TILES)]

        def first_product(t, cols, bank):
            acc = psum.tile([P, cols.stop - cols.start], F32, name="h_ps%d" % bank, tag="bank%d" % bank)
            for c in range(2):
                rows = slice(c * H + t * P, c * H + (t + 1) * P)
                nc.tensor.matmul_mx(
                    out=acc[:], lhsT=dq_w_dealt[:, rows].bitcast(FP8X4), lhsT_scale=first_plane[:, rows],
                    rhs=xq_w[:, cols].bitcast(FP8X4), rhs_scale=first_plane[:, 2 * H + cols.start : 2 * H + cols.stop],
                    start=(c == 0), stop=(c == 1),
                )
            nc.scalar.activation(ds[t][:, cols], acc[:], COPY, scale=row_factor[:, t : t + 1])

        first_product(0, HALVES[0], FIRST_EARLY_BANK)
        first_product(0, HALVES[1], 0)
        hz_b = keep.tile([P, HALF], U8, name="hz_b", tag="picked_words", align_bytes=64)
        nc.vector.tensor_copy(hz_b[:], x_sc[:].indirect(hz_l[:, LIST_HALVES[0]]))
        place_scale_rows(hz_plane[0], hz_b)
        hz_w = keep.tile([P, HALF], U32, name="hz_w", align_bytes=64)
        nc.vector.tensor_copy(hz_w[:], x_w[:].bitcast(U32).indirect(hz_l[:, LIST_HALVES[0]]))
        nc.vector.tensor_copy(pa[0][:], ds[0][:].indirect(n2_l[:]))
        nc.vector.tensor_copy(ds[0][:].indirect(n1_l[:]), pa[0][:])
        for t in range(1, TILES):
            first_product(t, slice(0, S), t)
            nc.scalar.activation(pa[t][:], ds[t][:].indirect(n2_l[:]), COPY)
            nc.vector.tensor_copy(ds[t][:].indirect(n1_l[:]), pa[t][:])

        w_plane = keep.tile([P, 2 * N], U8, name="w_plane", tag="dq_w_dealt", align_bytes=64)
        nc.gpsimd.tensor_copy(
            w_plane[:].bitcast(U32).rearrange("p (i t a b) -> p i t a b", i=2, t=TILES, b=RUN // 4),
            w_sc_raw[:].bitcast(U32).rearrange("p (i a t b) -> p i t a b", i=2, t=TILES, b=RUN // 4),
        )

        z_rows = keep.tile([P, 2, TILES, QUARTER], BF16, name="z_rows")
        for t in range(LAST):
            moved = keep.tile([P, HALF], F32, name="moved%d" % t)
            nc.scalar.activation(moved[:], ds[t][:].indirect(n3_l[:, LIST_HALVES[0]]), COPY, scale=0.5)
            nc.gpsimd.tensor_tensor(
                z_rows[:, :, t, :], ds[t][:, HALVES[0]].rearrange("p (q c) -> p q c", q=2),
                moved[:].rearrange("p (q c) -> p q c", q=2), ALU.subtract,
            )
        moved_late = [keep.tile([P, HALF], F32, name="moved_late%d" % t) for t in range(LAST)]

        def fetch_late(t):
            nc.scalar.activation(moved_late[t][:], ds[t][:].indirect(n3_l[:, LIST_HALVES[1]]), COPY, scale=0.5)

        fetch_late(0)
        for q in range(2):
            moved = keep.tile([P, QUARTER], F32, name="moved_q%d" % q)
            nc.scalar.activation(moved[:], ds[LAST][:].indirect(n3_l[:, LIST_QUARTERS[q]]), COPY, scale=0.5)
            nc.vector.tensor_tensor(z_rows[:, q, LAST, :], ds[LAST][:, QUARTERS[q]], moved[:], ALU.subtract)
        for t in range(1, LAST):
            fetch_late(t)

        h2 = [keep.tile([P, S], F32, name="h2_%d" % t) for t in range(TILES)]

        def w_pass(i, t, acc, words, scales):
            first = i * N + t * P
            nc.tensor.matmul_mx(
                out=acc, lhsT=w_dealt[:, 2 * first : 2 * (first + P)].bitcast(FP4X4),
                lhsT_scale=w_plane[:, first : first + P], rhs=words.bitcast(FP8X4), rhs_scale=scales,
                start=(i == 1), stop=(i == 0),
            )

        def interleaved(words, rows):
            return words.rearrange("p (c i) t -> p c t i", i=WALK), rows.rearrange("p t (c i) -> p c t i", i=WALK)

        quarter_ps = [
            psum.tile([P, QUARTER], F32, name="quarter_ps%d" % q, tag="bank%d" % QUARTER_BANKS[q]) for q in range(2)
        ]
        early_ps = {
            t: psum.tile([P, HALF], F32, name="early_ps%d" % t, tag="bank%d" % bank) for t, bank in EARLY_BANKS.items()
        }
        for q in range(2):
            w_pass(1, 0, quarter_ps[q][:], hz_w[:, QUARTERS[q]], hz_plane[0][:, QUARTERS[q]])
        for t in range(1, TILES):
            w_pass(1, t, early_ps[t][:], hz_w[:], hz_plane[0][:])
        z_in = [keep.tile([P, QUARTER, TILES], BF16, name="z_in%d" % q, tag="z_in%d" % q, align_bytes=64) for q in range(2)]
        z_w = keep.tile([P, HALF], U32, name="z_w", align_bytes=64)
        z_plane = keep.tile([P, HALF], U8, name="z_plane", tag="z_plane", align_bytes=64)
        for q in range(2):
            nc.vector.tensor_copy(*interleaved(z_in[q][:], z_rows[:, q]))
        for q in range(2):
            cols = QUARTERS[q]
            nc.vector.quantize_mx(
                out=z_w[:, cols].bitcast(FP8X4), scales=z_plane[:, cols], in_=z_in[q][:].rearrange("p c t -> p (c t)")
            )
            w_pass(0, 0, quarter_ps[q][:], z_w[:, cols], z_plane[:, cols])
            nc.scalar.copy(h2[0][:, cols], quarter_ps[q][:])
        for t in range(1, TILES):
            w_pass(0, t, early_ps[t][:], z_w[:], z_plane[:])
            nc.scalar.copy(h2[t][:, HALVES[0]], early_ps[t][:])

        hz_b_late = keep.tile([P, HALF], U8, name="hz_b_late", tag="pa%d" % LAST, align_bytes=64)
        nc.vector.tensor_copy(hz_b_late[:], x_sc[:].indirect(hz_l[:, LIST_HALVES[1]]))
        place_scale_rows(hz_plane[1], hz_b_late)
        hz_w_late = keep.tile([P, HALF], U32, name="hz_w_late", tag="z_in0", align_bytes=64)
        nc.vector.tensor_copy(hz_w_late[:], x_w[:].bitcast(U32).indirect(hz_l[:, LIST_HALVES[1]]))
        moved_late.append(keep.tile([P, HALF], F32, name="moved_last", tag="z_plane", align_bytes=64))
        fetch_late(LAST)

        ds2 = [keep.tile([P, S], F32, name="ds2_%d" % t) for t in range(LAST)]
        for q in range(2):
            nc.vector.tensor_copy(ds2[0][:].indirect(n4_l[:, LIST_QUARTERS[q]]), h2[0][:, QUARTERS[q]])
        for t in range(1, LAST):
            nc.vector.tensor_copy(ds2[t][:].indirect(n4_l[:, LIST_HALVES[0]]), h2[t][:, HALVES[0]])

        z_rows_late = keep.tile([P, TILES, HALF], BF16, name="z_rows_late", tag="z_in1", align_bytes=64)
        for t in range(TILES):
            nc.gpsimd.tensor_tensor(z_rows_late[:, t, :], ds[t][:, HALVES[1]], moved_late[t][:], ALU.subtract)
        z_in_late = keep.tile([P, HALF, TILES], BF16, name="z_in_late", align_bytes=64)
        nc.scalar.copy(*interleaved(z_in_late[:], z_rows_late[:]))
        z_w_late = keep.tile([P, HALF], U32, name="z_w_late", align_bytes=64)
        z_plane_late = keep.tile([P, HALF], U8, name="z_plane_late", align_bytes=64)
        nc.vector.quantize_mx(
            out=z_w_late[:].bitcast(FP8X4), scales=z_plane_late[:], in_=z_in_late[:].rearrange("p c t -> p (c t)")
        )
        for t in range(TILES):
            late_ps = psum.tile([P, HALF], F32, name="late_ps%d" % t, tag="bank%d" % LATE_BANKS[t])
            w_pass(1, t, late_ps[:], hz_w_late[:], hz_plane[1][:])
            w_pass(0, t, late_ps[:], z_w_late[:], z_plane_late[:])
            nc.scalar.copy(h2[t][:, HALVES[1]], late_ps[:])
        ds2.append(keep.tile([P, S], F32, name="ds2_last", tag="z_in1", align_bytes=64))
        nc.vector.tensor_copy(ds2[LAST][:].indirect(n4_l[:, LIST_HALVES[0]]), h2[LAST][:, HALVES[0]])

        out_rows = out.rearrange("(a t b) j -> t a b j", t=TILES, b=RUN)
        ds3 = [keep.tile([P, 2 * S], F32, name="ds3_%d" % t) for t in range(TILES)]
        st = [keep.tile([P, S], F32, name="st%d" % t) for t in range(TILES)]
        for t in range(TILES):
            tags = ("rise%d" % (t % 2), "excess%d" % (t % 2))
            nc.vector.tensor_copy(ds2[t][:].indirect(n4_l[:, LIST_HALVES[1]]), h2[t][:, HALVES[1]])
            rise = keep.tile([P, S], F32, name="rise%d" % t, tag=tags[t // 2])
            nc.gpsimd.tensor_tensor(rise[:], ds2[t][:], h2[t][:], ALU.subtract)
            excess = keep.tile([P, S], F32, name="excess%d" % t, tag=tags[1 - t // 2])
            nc.scalar.activation(excess[:], rise[:], RELU)
            nc.gpsimd.tensor_tensor(st[t][:], h2[t][:], excess[:], ALU.add)

        for t in range(LAST):
            nc.vector.tensor_copy(ds3[t][:].indirect(n5_l[:]), st[t][:])
            result = keep.tile([P, S], F32, name="result%d" % t)
            nc.gpsimd.tensor_tensor(result[:], st[t][:], ds3[t][:, 0:S], ALU.subtract)
            nc.sync.dma_start(out_rows[t], result[:])
        nc.vector.tensor_copy(ds3[LAST][:].indirect(n5_l[:]), st[LAST][:])
        for u, queue in enumerate((nc.sync, nc.scalar)):
            result = keep.tile([P, HALF], F32, name="last_result%d" % u)
            nc.vector.tensor_tensor(result[:], st[LAST][:, HALVES[u]], ds3[LAST][:, HALVES[u]], ALU.subtract)
            queue.dma_start(out_rows[LAST][:, :, HALVES[u]], result[:])
